import numpy as np
import ml_dtypes


def mxq(x, axis, fmt="e4m3"):
    dtype, down = {"e4m3": (ml_dtypes.float8_e4m3fn, 7), "e5m2": (ml_dtypes.float8_e5m2, 14)}[fmt]
    v = np.moveaxis(np.asarray(x, np.float32).astype(ml_dtypes.bfloat16).astype(np.float64), axis, -1)
    blocks = v.reshape(v.shape[:-1] + (-1, 32))
    amax = np.abs(blocks).max(-1, keepdims=True)
    byte = np.maximum(np.where(amax > 0, np.frexp(amax)[1] - 1 + 127, 0) - down, 1)
    scale = np.exp2(byte - 127.0)
    codes = (blocks / scale).astype(np.float32).astype(dtype).astype(np.float64)
    return np.moveaxis((codes * scale).reshape(v.shape), -1, axis)


WIDE = False


def mx_kscale(k):
    if not WIDE:
        return np.ones(k)
    levels = np.array([10, -10, 5, -5, 0])
    if k % 512:
        return np.exp2(np.random.permutation(np.resize(levels, k // 32))).repeat(32)
    a = np.empty((k // 512, 16))
    for p in range(k // 512):
        a[p, :8] = np.random.permutation(np.resize(levels, 8))
        for g in range(8):
            far = levels[np.abs(levels - a[p, g]) >= 10]
            a[p, g + 8] = far[np.random.randint(len(far))]
    return np.exp2(a.ravel()).repeat(32)


def f64(x):
    return np.asarray(x).astype(np.float64)


def striped(idx):
    return np.tile(np.asarray(idx).reshape(-1, 16).T, (8, 1)).astype(np.uint16)


def unstriped(offs):
    return offs[:16].T.reshape(-1).astype(np.int64)


E2M1 = np.array([0.0, 0.5, 1.0, 1.5, 2.0, 3.0, 4.0, 6.0, -0.0, -0.5, -1.0, -1.5, -2.0, -3.0, -4.0, -6.0])


def pack_weight(w, fmt):
    k, n = w.shape
    w = f64(np.asarray(w, np.float32).astype(ml_dtypes.bfloat16)).reshape(k // 32, 32, n)
    amax = np.abs(w).max(1)
    if fmt == "e4m3":
        byte = np.frexp(amax)[1] - 1 + 127 - 7
    else:
        mant, ex = np.frexp(amax / 6.0)
        byte = np.where(mant > 0.5, ex, ex - 1) + 127
    byte = np.clip(np.where(amax > 0, byte, 1), 1, 254)
    scaled = (w * np.exp2(127.0 - byte)[:, None, :]).reshape(k, n).astype(np.float32)
    by_word = np.ascontiguousarray(scaled.reshape(k // 512, 128, 4, n).transpose(0, 1, 3, 2))
    if fmt == "e4m3":
        words = by_word.astype(ml_dtypes.float8_e4m3fn).view(np.uint8)
    else:
        c = by_word.astype(ml_dtypes.float4_e2m1fn).view(np.uint8) & 0xF
        words = (c[..., 0::2] | (c[..., 1::2] << 4)).reshape(k // 512, 128, 2 * n)
    return np.ascontiguousarray(words), np.ascontiguousarray(byte.astype(np.uint8).reshape(k // 512, 16, n))


def unpack_weight(words, scales, fmt):
    g, _, n = scales.shape
    words = np.ascontiguousarray(words).reshape(g, 128, n, -1)
    if fmt == "e4m3":
        vals = words.view(ml_dtypes.float8_e4m3fn).astype(np.float64)
    else:
        nib = np.empty((g, 128, n, 4), np.uint8)
        nib[..., 0::2] = words & 0xF
        nib[..., 1::2] = words >> 4
        vals = E2M1[nib]
    vals = vals * np.repeat(np.exp2(scales.astype(np.float64) - 127.0), 8, axis=1)[..., None]
    return vals.transpose(0, 1, 3, 2).reshape(g * 512, n)


D, T, I, Q, E, J, M = 512, 2048, 512, 128, 512, 512, 512


def setup_inputs():
    n = np.random.standard_normal
    idx = np.random.permutation(T)[:I]
    fd = mx_kscale(D)
    fj = mx_kscale(J)
    fi = mx_kscale(I)
    fm = mx_kscale(M)
    ti = np.ones(T)
    ti[idx] = fi
    keysp = pack_weight(n((D, T)) / fd[:, None], "e4m3")
    return {
        "query": (n((D, Q)) * 0.4 / np.sqrt(D) * fd[:, None]).astype(np.float32),
        "ckey": (n((D, J)) / fd[:, None]).astype(np.float32),
        "cval": (n((J, E)) / fj[:, None]).astype(np.float32),
        "keys_words": keysp[0],
        "keys_scales": keysp[1],
        "vals": (n((E, T)) / ti).astype(np.float32),
        "wkey": (n((D, M)) / fd[:, None]).astype(np.float32),
        "wval": (n((M, E)) / fm[:, None]).astype(np.float32),
        "gc": (np.random.uniform(0.2, 1.0, (Q, 1))).astype(np.float32),
        "gs": (np.random.uniform(0.2, 1.0, (Q, 1))).astype(np.float32),
        "gw": (np.random.uniform(0.2, 1.0, (Q, 1))).astype(np.float32),
        "cf": (np.random.uniform(0.5, 2.0, (1, J)) * fj).astype(np.float32),
        "size": (np.random.uniform(0.5, 2.0, (1, I)) * fi).astype(np.float32),
        "mf": (np.random.uniform(0.5, 2.0, (1, M)) * fm).astype(np.float32),
        "offs": striped(idx),
    }


def reference(query, ckey, cval, keys_words, keys_scales, vals, wkey, wval, gc, gs, gw, cf, size, mf, offs):
    idx = unstriped(offs)
    keysu = unpack_weight(keys_words, keys_scales, "e4m3")
    queryq = mxq(f64(query), 0, "e4m3")
    ckeyq = mxq(f64(ckey), 0, "e4m3")
    a = queryq.T @ ckeyq
    keysidxg = keysu[:, idx]
    b = queryq.T @ keysidxg
    wkeyq = mxq(f64(wkey), 0, "e4m3")
    s = queryq.T @ wkeyq
    pc = np.exp(a - np.max(a, axis=1, keepdims=True))
    wc = pc * f64(gc) * f64(cf) / np.sum(pc, axis=1, keepdims=True)
    wtc = wc.T
    ps = np.exp(b - np.max(b, axis=1, keepdims=True))
    ws = ps * f64(gs) * f64(size) / np.sum(ps, axis=1, keepdims=True)
    wts = ws.T
    pw = np.exp(s - np.max(s, axis=1, keepdims=True))
    ww = pw * f64(gw) * f64(mf) / np.sum(pw, axis=1, keepdims=True)
    wtw = ww.T
    vt = f64(vals)[:, idx].T
    wtcq = mxq(wtc, 0, "e4m3")
    cvalq = mxq(f64(cval), 0, "e4m3")
    wtsq = mxq(wts, 0, "e4m3")
    vtq = mxq(vt, 0, "e4m3")
    wtwq = mxq(wtw, 0, "e4m3")
    wvalq = mxq(f64(wval), 0, "e4m3")
    o = wtcq.T @ cvalq + wtsq.T @ vtq + wtwq.T @ wvalq
    return o

@@ -1,0 +1,193 @@
+from contextlib import ExitStack
+
+import concourse.mybir as mybir
+from concourse.masks import make_identity
+
+D, T, I, Q, E = 512, 2048, 512, 128, 512
+FLOPS = 6 * 2 * 512 * 128 * 512
+
+F32 = mybir.dt.float32
+BF16 = mybir.dt.bfloat16
+I32 = mybir.dt.int32
+U32 = mybir.dt.uint32
+U16 = mybir.dt.uint16
+U8 = mybir.dt.uint8
+FP8X4 = mybir.dt.float8_e4m3fn_x4
+ALU = mybir.AluOpType
+ACT = mybir.ActivationFunctionType
+AX = mybir.AxisListType
+
+P = 128
+PACK = 4
+N = 512
+HALF = 256
+VEC_ROW0 = 8
+OUT_CHUNKS = ((0, 256), (256, 384), (384, 512))
+
+
+def tile_attend_nsa_branches_kernel(tc, query, ckey, cval, keys_words, keys_scales, vals, wkey, wval,
+                                     gc, gs, gw, cf, size, mf, offs, out):
+    nc = tc.nc
+    with ExitStack() as ctx:
+        keep = ctx.enter_context(tc.tile_pool(name="keep", bufs=1))
+        psum = ctx.enter_context(tc.psum_pool(name="psum", bufs=1))
+        on_vector, on_scalar = nc.vector.tensor_copy, nc.scalar.copy
+
+        def sbuf(shape, dtype, name, reuses=None):
+            return keep.tile(shape, dtype, name=name, tag=reuses or name, align_bytes=64)
+
+        def load_rows(src, c0, c1, name):
+            raw = sbuf([P, PACK, c1 - c0], F32, name)
+            nc.sync.dma_start(out=raw[:], in_=src.rearrange("(p j) w -> p j w", j=PACK)[:, :, c0:c1])
+            return raw
+
+        def interleave(pieces, name):
+            grouped = sbuf([P, sum(c1 - c0 for copy, raw, c0, c1 in pieces), PACK], BF16, name)
+            a = 0
+            for copy, raw, c0, c1 in pieces:
+                copy(out=grouped[:, a : a + c1 - c0, :].rearrange("p (c i) t -> p c t i", i=4),
+                     in_=raw[:, :, c0:c1].rearrange("p t (c i) -> p c t i", i=4))
+                a = a + c1 - c0
+            return grouped
+
+        def quantize(grouped, name, codes=None):
+            width = grouped.shape[1]
+            if codes is None:
+                codes = sbuf([P, width], U32, name + "_codes")[:]
+            scales = sbuf([P, width], U8, name + "_scales")[:]
+            nc.vector.quantize_mx(out=codes.bitcast(FP8X4), scales=scales,
+                                  in_=grouped[:].rearrange("p w j -> p (w j)"))
+            return codes, scales
+
+        def multiply(acc, lhs, rhs, start, stop):
+            nc.tensor.matmul_mx(out=acc, lhsT=lhs[0].bitcast(FP8X4), lhsT_scale=lhs[1],
+                                rhs=rhs[0].bitcast(FP8X4), rhs_scale=rhs[1], start=start, stop=stop)
+
+        def turn_pairs(rows_bf16, grouped):
+            words = rows_bf16.bitcast(F32)
+            turned = psum.tile([P, 2, P], F32, name="turned", tag="turn", bufs=3)
+            for u in range(2):
+                nc.tensor.transpose(turned[:, u, :], words[:, u : 2 * P : 2], ident[:])
+            nc.scalar.copy(out=grouped.bitcast(F32), in_=turned[:].rearrange("p u r -> p r u"))
+
+        ident = sbuf([P, P], F32, "ident")
+        make_identity(nc, ident[:])
+        key_scales = sbuf([P, T], U8, "key_scales")
+        nc.vector.memset(key_scales[:].bitcast(I32), 0)
+        vec_rows = sbuf([P, P], F32, "vec_rows")
+        nc.vector.memset(vec_rows[:], 0.0)
+        for quad in range(4):
+            nc.gpsimd.dma_start(out=key_scales[32 * quad : 32 * quad + 4, :].bitcast(I32),
+                                in_=keys_scales[0, 4 * quad : 4 * quad + 4, :].bitcast(I32))
+        for n, (g, f) in enumerate(((gc, cf), (gs, size), (gw, mf))):
+            r0 = VEC_ROW0 + 5 * n
+            nc.scalar.dma_start(out=vec_rows[r0 : r0 + 4, :], in_=f.rearrange("o (r n) -> (o r) n", n=P))
+            nc.scalar.dma_start(out=vec_rows[r0 + 4 : r0 + 5, :], in_=g.rearrange("q o -> o q"))
+
+        q_raw = load_rows(query, 0, Q, "q_raw")
+        offsets = keep.tile([P, I // 16], U16, name="offsets")
+        nc.sync.dma_start(offsets[:], offs)
+        ck_raw = [load_rows(ckey, c0, c0 + HALF, "ck_raw%d" % c0) for c0 in (0, HALF)]
+        key_words = sbuf([P, T], U32, "key_words")
+        nc.sync.dma_start(out=key_words[:].bitcast(I32),
+                          in_=keys_words[0].rearrange("p n t -> p (n t)").bitcast(I32))
+        wk_raw = [load_rows(wkey, c0, c0 + HALF, "wk_raw%d" % c0) for c0 in (0, HALF)]
+        pools = []
+        for b in range(E // P):
+            pool_b = sbuf([P, T], F32, "vals%d" % b)
+            nc.sync.dma_start(out=pool_b[:], in_=vals[b * P : (b + 1) * P, :])
+            pools.append(pool_b)
+        cv_raw = [load_rows(cval, c0, c0 + HALF, "cv_raw%d" % c0) for c0 in (0, HALF)]
+        wv_raw = [load_rows(wval, c0, c1, "wv_raw%d" % c0) for c0, c1 in OUT_CHUNKS]
+
+        vec_turned = psum.tile([P, P], F32, name="vec_turned", tag="turn", bufs=3)
+        nc.tensor.transpose(vec_turned[:], vec_rows[:], ident[:])
+        vec_cols = sbuf([P, 16], F32, "vec_cols")
+        nc.scalar.copy(out=vec_cols[:], in_=vec_turned[:, VEC_ROW0 : VEC_ROW0 + 16])
+        factors = []
+        for n in range(3):
+            spread = psum.tile([P, PACK, P], F32, name="spread%d" % n, tag="acc%d" % n)
+            for t in range(PACK):
+                nc.tensor.transpose(spread[:, t, :], vec_cols[:, 5 * n + t : 5 * n + t + 1].to_broadcast([P, P]),
+                                    ident[:])
+            factor = sbuf([P, N], F32, "factor%d" % n)
+            nc.scalar.activation(out=factor[:], in_=spread[:].rearrange("p t s -> p (t s)"), func=ACT.Copy,
+                                 scale=vec_cols[:, 5 * n + 4 : 5 * n + 5])
+            factors.append(factor)
+
+        def softmax(n, keys_mx, probs_reuses=None):
+            scores = psum.tile([P, N], F32, name="scores%d" % n, tag="scores", bufs=2)
+            multiply(scores[:], q_mx, keys_mx, True, True)
+            neg_max = sbuf([P, 1], F32, "neg_max%d" % n)
+            nc.vector.tensor_reduce(out=neg_max[:], in_=scores[:], axis=AX.X, op=ALU.max, negate=True)
+            probs = sbuf([P, N], F32, "probs%d" % n, probs_reuses)
+            total = sbuf([P, 1], F32, "total%d" % n)
+            nc.scalar.activation(out=probs[:], in_=scores[:], func=ACT.Exp, bias=neg_max[:], accum_out=total[:])
+            inverse = sbuf([P, 1], F32, "inverse%d" % n)
+            nc.vector.reciprocal(out=inverse[:], in_=total[:])
+            return probs, inverse
+
+        def weigh(n, probs, inverse, reuses=None):
+            w_rows = sbuf([P, N], BF16, "w_rows%d" % n, reuses)
+            nc.vector.scalar_tensor_tensor(out=w_rows[:], in0=probs[:], scalar=inverse[:], in1=factors[n][:],
+                                           op0=ALU.mult, op1=ALU.mult)
+            grouped = sbuf([P, Q, PACK], BF16, "w_grp%d" % n)
+            turn_pairs(w_rows[:], grouped[:])
+            return grouped
+
+        def gather_values(b, grouped):
+            picked = sbuf([P, I], BF16, "picked%d" % b)
+            nc.vector.tensor_copy(out=picked[:], in_=pools[b][:].indirect(offsets[:]))
+            turn_pairs(picked[:], grouped)
+
+        q_mx = quantize(interleave([(on_vector, q_raw, 0, Q)], "q_grp"), "q")
+        ck_mx = quantize(interleave([(on_vector, raw, 0, HALF) for raw in ck_raw], "ck_grp"), "ck")
+        sk_scales = sbuf([P, I], U8, "sk_scales", "ck_raw%d" % HALF)
+        sk_codes = sbuf([P, I], U32, "sk_codes")
+        nc.vector.tensor_copy(out=sk_scales[:], in_=key_scales[:].indirect(offsets[:]))
+        nc.vector.tensor_copy(out=sk_codes[:], in_=key_words[:].indirect(offsets[:]))
+        wk_grp = interleave([(on_vector, wk_raw[0], 0, HALF), (on_scalar, wk_raw[1], 0, HALF)], "wk_grp")
+        soft_c = softmax(0, ck_mx, "wk_raw%d" % HALF)
+        soft_s = softmax(1, (sk_codes[:], sk_scales[:]))
+        ws_grp = weigh(1, *soft_s)
+        soft_w = softmax(2, quantize(wk_grp, "wk"))
+
+        vt_grp01 = sbuf([P, HALF, PACK], BF16, "vt_grp01")
+        vt_grp2 = sbuf([P, P, PACK], BF16, "vt_grp2")
+        gather_values(0, vt_grp01[:, 0:P, :])
+        wc_grp = weigh(0, *soft_c, "vals0")
+        gather_values(1, vt_grp01[:, P:HALF, :])
+        codes1 = sbuf([P, 2 * Q], U32, "codes1", "vals1")
+        wc_mx = quantize(wc_grp, "wc", codes1[:, 0:Q])
+        ws_mx = quantize(ws_grp, "ws", codes1[:, Q : 2 * Q])
+        gather_values(2, vt_grp2[:])
+        ww_grp = weigh(2, *soft_w, "vals2")
+        vt_mx = [quantize(vt_grp01, "vt01", sbuf([P, HALF], U32, "codes2", "probs2")[:])]
+        cv_grp0 = interleave([(on_scalar, cv_raw[0], 0, HALF)], "cv_grp0")
+        vt_grp3 = sbuf([P, P, PACK], BF16, "vt_grp3", "cv_raw0")
+        gather_values(3, vt_grp3[:])
+        codes3 = sbuf([P, Q + P], U32, "codes3", "vals3")
+        ww_mx = quantize(ww_grp, "ww", codes3[:, 0:Q])
+        vt_mx.append(quantize(vt_grp2, "vt2", codes3[:, Q : Q + P]))
+        vt_mx.append(quantize(vt_grp3, "vt3"))
+
+        accs = [psum.tile([P, c1 - c0], F32, name="acc%d" % k, tag="acc%d" % k)
+                for k, (c0, c1) in enumerate(OUT_CHUNKS)]
+        for acc, v_mx in zip(accs, vt_mx):
+            multiply(acc[:], ws_mx, v_mx, True, False)
+
+        multiply(accs[0][:], wc_mx, quantize(cv_grp0, "cv0"), False, False)
+        multiply(accs[1][:], wc_mx, quantize(interleave([(on_vector, cv_raw[1], 0, P)], "cv_grp1"), "cv1"),
+                 False, False)
+        multiply(accs[2][:], wc_mx, quantize(interleave([(on_scalar, cv_raw[1], P, HALF)], "cv_grp2"), "cv2"),
+                 False, False)
+
+        wv_grp = [interleave([(on_vector, wv_raw[0], 0, P), (on_scalar, wv_raw[0], P, HALF)], "wv_grp0"),
+                  interleave([(on_scalar, wv_raw[1], 0, P)], "wv_grp1"),
+                  interleave([(on_vector, wv_raw[2], 0, P)], "wv_grp2")]
+        wv_mx = [quantize(grouped, "wv%d" % k) for k, grouped in enumerate(wv_grp)]
+        for acc, v_mx, (c0, c1) in zip(accs, wv_mx, OUT_CHUNKS):
+            multiply(acc[:], ww_mx, v_mx, False, True)
+            result = sbuf([P, c1 - c0], F32, "result%d" % c0)
+            nc.scalar.copy(out=result[:], in_=acc[:])
+            nc.sync.dma_start(out=out[:, c0:c1], in_=result[:])

@@ -59,6 +59,9 @@ def tile_attend_nsa_branches_kernel(tc, query, ckey, cval, keys_words, keys_scal
                                   in_=grouped[:].rearrange("p w j -> p (w j)"))
             return codes, scales
 
+        def columns(mx, c0, c1):
+            return mx[0][:, c0:c1], mx[1][:, c0:c1]
+
         def multiply(acc, lhs, rhs, start, stop):
             nc.tensor.matmul_mx(out=acc, lhsT=lhs[0].bitcast(FP8X4), lhsT_scale=lhs[1],
                                 rhs=rhs[0].bitcast(FP8X4), rhs_scale=rhs[1], start=start, stop=stop)
@@ -70,28 +73,24 @@ def tile_attend_nsa_branches_kernel(tc, query, ckey, cval, keys_words, keys_scal
                 nc.tensor.transpose(turned[:, u, :], words[:, u : 2 * P : 2], ident[:])
             nc.scalar.copy(out=grouped.bitcast(F32), in_=turned[:].rearrange("p u r -> p r u"))
 
+        key_scales = sbuf([P, T], U8, "key_scales")
+        nc.gpsimd.memset(key_scales[:].bitcast(I32), 0)
+        vec_rows = sbuf([P, P], F32, "vec_rows")
+        nc.gpsimd.memset(vec_rows[:], 0.0)
         ident = sbuf([P, P], F32, "ident")
         make_identity(nc, ident[:])
-        key_scales = sbuf([P, T], U8, "key_scales")
-        nc.vector.memset(key_scales[:].bitcast(I32), 0)
-        vec_rows = sbuf([P, P], F32, "vec_rows")
-        nc.vector.memset(vec_rows[:], 0.0)
         for quad in range(4):
-            nc.gpsimd.dma_start(out=key_scales[32 * quad : 32 * quad + 4, :].bitcast(I32),
+            nc.scalar.dma_start(out=key_scales[32 * quad : 32 * quad + 4, :].bitcast(I32),
                                 in_=keys_scales[0, 4 * quad : 4 * quad + 4, :].bitcast(I32))
-        for n, (g, f) in enumerate(((gc, cf), (gs, size), (gw, mf))):
-            r0 = VEC_ROW0 + 5 * n
-            nc.scalar.dma_start(out=vec_rows[r0 : r0 + 4, :], in_=f.rearrange("o (r n) -> (o r) n", n=P))
-            nc.scalar.dma_start(out=vec_rows[r0 + 4 : r0 + 5, :], in_=g.rearrange("q o -> o q"))
 
         q_raw = load_rows(query, 0, Q, "q_raw")
         offsets = keep.tile([P, I // 16], U16, name="offsets")
         nc.sync.dma_start(offsets[:], offs)
-        ck_raw = [load_rows(ckey, c0, c0 + HALF, "ck_raw%d" % c0) for c0 in (0, HALF)]
+        ck_raw = load_rows(ckey, 0, N, "ck_raw")
         key_words = sbuf([P, T], U32, "key_words")
         nc.sync.dma_start(out=key_words[:].bitcast(I32),
                           in_=keys_words[0].rearrange("p n t -> p (n t)").bitcast(I32))
-        wk_raw = [load_rows(wkey, c0, c0 + HALF, "wk_raw%d" % c0) for c0 in (0, HALF)]
+        wk_raw = load_rows(wkey, 0, N, "wk_raw")
         pools = []
         for b in range(E // P):
             pool_b = sbuf([P, T], F32, "vals%d" % b)
@@ -99,6 +98,44 @@ def tile_attend_nsa_branches_kernel(tc, query, ckey, cval, keys_words, keys_scal
             pools.append(pool_b)
         cv_raw = [load_rows(cval, c0, c0 + HALF, "cv_raw%d" % c0) for c0 in (0, HALF)]
         wv_raw = [load_rows(wval, c0, c1, "wv_raw%d" % c0) for c0, c1 in OUT_CHUNKS]
+
+        def softmax(n, keys_mx, probs_reuses=None):
+            scores = psum.tile([P, N], F32, name="scores%d" % n, tag="scores", bufs=2)
+            multiply(scores[:], q_mx, keys_mx, True, True)
+            neg_max = sbuf([P, 1], F32, "neg_max%d" % n)
+            nc.vector.tensor_reduce(out=neg_max[:], in_=scores[:], axis=AX.X, op=ALU.max, negate=True)
+            probs = sbuf([P, N], F32, "probs%d" % n, probs_reuses)
+            total = sbuf([P, 1], F32, "total%d" % n)
+            nc.scalar.activation(out=probs[:], in_=scores[:], func=ACT.Exp, bias=neg_max[:], accum_out=total[:])
+            inverse = sbuf([P, 1], F32, "inverse%d" % n)
+            nc.vector.reciprocal(out=inverse[:], in_=total[:])
+            return probs, inverse
+
+        def weigh(n, probs, inverse, grouped):
+            w_rows = sbuf([P, N], BF16, "w_rows%d" % n)
+            nc.vector.scalar_tensor_tensor(out=w_rows[:], in0=probs[:], scalar=inverse[:], in1=factors[n][:],
+                                           op0=ALU.mult, op1=ALU.mult)
+            turn_pairs(w_rows[:], grouped)
+
+        def gather_values(b, grouped):
+            picked = sbuf([P, I], BF16, "picked%d" % b)
+            nc.vector.tensor_copy(out=picked[:], in_=pools[b][:].indirect(offsets[:]))
+            turn_pairs(picked[:], grouped)
+
+        q_mx = quantize(interleave([(on_vector, q_raw, 0, Q)], "q_grp"), "q")
+        ck_grp = interleave([(on_vector, ck_raw, 0, HALF), (on_scalar, ck_raw, HALF, N)], "ck_grp")
+        for n, (g, f) in enumerate(((gc, cf), (gs, size), (gw, mf))):
+            r0 = VEC_ROW0 + 5 * n
+            nc.scalar.dma_start(out=vec_rows[r0 : r0 + 4, :], in_=f.rearrange("o (r n) -> (o r) n", n=P))
+            nc.scalar.dma_start(out=vec_rows[r0 + 4 : r0 + 5, :], in_=g.rearrange("q o -> o q"))
+        ck_mx = quantize(ck_grp, "ck")
+        sk_scales = sbuf([P, I], U8, "sk_scales")
+        sk_codes = sbuf([P, I], U32, "sk_codes")
+        nc.vector.tensor_copy(out=sk_scales[:], in_=key_scales[:].indirect(offsets[:]))
+        nc.vector.tensor_copy(out=sk_codes[:], in_=key_words[:].indirect(offsets[:]))
+        wk_grp = interleave([(on_vector, wk_raw, 0, HALF), (on_scalar, wk_raw, HALF, N)], "wk_grp")
+        soft_c = softmax(0, ck_mx)
+        soft_s = softmax(1, (sk_codes[:], sk_scales[:]), "wk_raw")
 
         vec_turned = psum.tile([P, P], F32, name="vec_turned", tag="turn", bufs=3)
         nc.tensor.transpose(vec_turned[:], vec_rows[:], ident[:])
@@ -115,61 +152,23 @@ def tile_attend_nsa_branches_kernel(tc, query, ckey, cval, keys_words, keys_scal
                                  scale=vec_cols[:, 5 * n + 4 : 5 * n + 5])
             factors.append(factor)
 
-        def softmax(n, keys_mx, probs_reuses=None):
-            scores = psum.tile([P, N], F32, name="scores%d" % n, tag="scores", bufs=2)
-            multiply(scores[:], q_mx, keys_mx, True, True)
-            neg_max = sbuf([P, 1], F32, "neg_max%d" % n)
-            nc.vector.tensor_reduce(out=neg_max[:], in_=scores[:], axis=AX.X, op=ALU.max, negate=True)
-            probs = sbuf([P, N], F32, "probs%d" % n, probs_reuses)
-            total = sbuf([P, 1], F32, "total%d" % n)
-            nc.scalar.activation(out=probs[:], in_=scores[:], func=ACT.Exp, bias=neg_max[:], accum_out=total[:])
-            inverse = sbuf([P, 1], F32, "inverse%d" % n)
-            nc.vector.reciprocal(out=inverse[:], in_=total[:])
-            return probs, inverse
-
-        def weigh(n, probs, inverse, reuses=None):
-            w_rows = sbuf([P, N], BF16, "w_rows%d" % n, reuses)
-            nc.vector.scalar_tensor_tensor(out=w_rows[:], in0=probs[:], scalar=inverse[:], in1=factors[n][:],
-                                           op0=ALU.mult, op1=ALU.mult)
-            grouped = sbuf([P, Q, PACK], BF16, "w_grp%d" % n)
-            turn_pairs(w_rows[:], grouped[:])
-            return grouped
-
-        def gather_values(b, grouped):
-            picked = sbuf([P, I], BF16, "picked%d" % b)
-            nc.vector.tensor_copy(out=picked[:], in_=pools[b][:].indirect(offsets[:]))
-            turn_pairs(picked[:], grouped)
-
-        q_mx = quantize(interleave([(on_vector, q_raw, 0, Q)], "q_grp"), "q")
-        ck_mx = quantize(interleave([(on_vector, raw, 0, HALF) for raw in ck_raw], "ck_grp"), "ck")
-        sk_scales = sbuf([P, I], U8, "sk_scales", "ck_raw%d" % HALF)
-        sk_codes = sbuf([P, I], U32, "sk_codes")
-        nc.vector.tensor_copy(out=sk_scales[:], in_=key_scales[:].indirect(offsets[:]))
-        nc.vector.tensor_copy(out=sk_codes[:], in_=key_words[:].indirect(offsets[:]))
-        wk_grp = interleave([(on_vector, wk_raw[0], 0, HALF), (on_scalar, wk_raw[1], 0, HALF)], "wk_grp")
-        soft_c = softmax(0, ck_mx, "wk_raw%d" % HALF)
-        soft_s = softmax(1, (sk_codes[:], sk_scales[:]))
-        ws_grp = weigh(1, *soft_s)
+        first = sbuf([P, 4 * P, PACK], BF16, "first")
+        second = sbuf([P, 2 * P, PACK], BF16, "second")
+        weigh(1, *soft_s, first[:, P : 2 * P, :])
         soft_w = softmax(2, quantize(wk_grp, "wk"))
 
-        vt_grp01 = sbuf([P, HALF, PACK], BF16, "vt_grp01")
-        vt_grp2 = sbuf([P, P, PACK], BF16, "vt_grp2")
-        gather_values(0, vt_grp01[:, 0:P, :])
-        wc_grp = weigh(0, *soft_c, "vals0")
-        gather_values(1, vt_grp01[:, P:HALF, :])
-        codes1 = sbuf([P, 2 * Q], U32, "codes1", "vals1")
-        wc_mx = quantize(wc_grp, "wc", codes1[:, 0:Q])
-        ws_mx = quantize(ws_grp, "ws", codes1[:, Q : 2 * Q])
-        gather_values(2, vt_grp2[:])
-        ww_grp = weigh(2, *soft_w, "vals2")
-        vt_mx = [quantize(vt_grp01, "vt01", sbuf([P, HALF], U32, "codes2", "probs2")[:])]
+        gather_values(0, first[:, 2 * P : 3 * P, :])
+        weigh(0, *soft_c, first[:, 0:P, :])
+        gather_values(1, first[:, 3 * P : 4 * P, :])
+        gather_values(2, second[:, P : 2 * P, :])
+        first_mx = quantize(first, "first", sbuf([P, 4 * P], U32, "first_codes", "vals2")[:])
+        weigh(2, *soft_w, second[:, 0:P, :])
         cv_grp0 = interleave([(on_scalar, cv_raw[0], 0, HALF)], "cv_grp0")
-        vt_grp3 = sbuf([P, P, PACK], BF16, "vt_grp3", "cv_raw0")
-        gather_values(3, vt_grp3[:])
-        codes3 = sbuf([P, Q + P], U32, "codes3", "vals3")
-        ww_mx = quantize(ww_grp, "ww", codes3[:, 0:Q])
-        vt_mx.append(quantize(vt_grp2, "vt2", codes3[:, Q : Q + P]))
-        vt_mx.append(quantize(vt_grp3, "vt3"))
+        third = sbuf([P, P, PACK], BF16, "third", "cv_raw0")
+        gather_values(3, third[:])
+        second_mx = quantize(second, "second", sbuf([P, 2 * P], U32, "second_codes", "vals3")[:])
+        wc_mx, ws_mx, ww_mx = columns(first_mx, 0, P), columns(first_mx, P, 2 * P), columns(second_mx, 0, P)
+        vt_mx = [columns(first_mx, 2 * P, 4 * P), columns(second_mx, P, 2 * P), quantize(third, "third")]
 
         accs = [psum.tile([P, c1 - c0], F32, name="acc%d" % k, tag="acc%d" % k)
                 for k, (c0, c1) in enumerate(OUT_CHUNKS)]

@@ -41,8 +41,8 @@ def tile_attend_nsa_branches_kernel(tc, query, ckey, cval, keys_words, keys_scal
             nc.sync.dma_start(out=raw[:], in_=src.rearrange("(p j) w -> p j w", j=PACK)[:, :, c0:c1])
             return raw
 
-        def interleave(pieces, name):
-            grouped = sbuf([P, sum(c1 - c0 for copy, raw, c0, c1 in pieces), PACK], BF16, name)
+        def interleave(pieces, name, reuses=None):
+            grouped = sbuf([P, sum(c1 - c0 for copy, raw, c0, c1 in pieces), PACK], BF16, name, reuses)
             a = 0
             for copy, raw, c0, c1 in pieces:
                 copy(out=grouped[:, a : a + c1 - c0, :].rearrange("p (c i) t -> p c t i", i=4),
@@ -73,12 +73,15 @@ def tile_attend_nsa_branches_kernel(tc, query, ckey, cval, keys_words, keys_scal
                 nc.tensor.transpose(turned[:, u, :], words[:, u : 2 * P : 2], ident[:])
             nc.scalar.copy(out=grouped.bitcast(F32), in_=turned[:].rearrange("p u r -> p r u"))
 
-        key_scales = sbuf([P, T], U8, "key_scales")
-        nc.gpsimd.memset(key_scales[:].bitcast(I32), 0)
         vec_rows = sbuf([P, P], F32, "vec_rows")
         nc.gpsimd.memset(vec_rows[:], 0.0)
+        key_scales = sbuf([P, T], U8, "key_scales")
+        nc.gpsimd.memset(key_scales[:].bitcast(I32), 0)
         ident = sbuf([P, P], F32, "ident")
         make_identity(nc, ident[:])
+        for n, f in enumerate((cf, size, mf)):
+            r0 = VEC_ROW0 + PACK * n
+            nc.scalar.dma_start(out=vec_rows[r0 : r0 + PACK, :], in_=f.rearrange("o (r n) -> (o r) n", n=P))
         for quad in range(4):
             nc.scalar.dma_start(out=key_scales[32 * quad : 32 * quad + 4, :].bitcast(I32),
                                 in_=keys_scales[0, 4 * quad : 4 * quad + 4, :].bitcast(I32))
@@ -99,21 +102,20 @@ def tile_attend_nsa_branches_kernel(tc, query, ckey, cval, keys_words, keys_scal
         cv_raw = [load_rows(cval, c0, c0 + HALF, "cv_raw%d" % c0) for c0 in (0, HALF)]
         wv_raw = [load_rows(wval, c0, c1, "wv_raw%d" % c0) for c0, c1 in OUT_CHUNKS]
 
-        def softmax(n, keys_mx, probs_reuses=None):
+        def softmax(n, keys_mx, probs):
             scores = psum.tile([P, N], F32, name="scores%d" % n, tag="scores", bufs=2)
             multiply(scores[:], q_mx, keys_mx, True, True)
             neg_max = sbuf([P, 1], F32, "neg_max%d" % n)
             nc.vector.tensor_reduce(out=neg_max[:], in_=scores[:], axis=AX.X, op=ALU.max, negate=True)
-            probs = sbuf([P, N], F32, "probs%d" % n, probs_reuses)
             total = sbuf([P, 1], F32, "total%d" % n)
-            nc.scalar.activation(out=probs[:], in_=scores[:], func=ACT.Exp, bias=neg_max[:], accum_out=total[:])
+            nc.scalar.activation(out=probs, in_=scores[:], func=ACT.Exp, bias=neg_max[:], accum_out=total[:])
             inverse = sbuf([P, 1], F32, "inverse%d" % n)
             nc.vector.reciprocal(out=inverse[:], in_=total[:])
             return probs, inverse
 
         def weigh(n, probs, inverse, grouped):
             w_rows = sbuf([P, N], BF16, "w_rows%d" % n)
-            nc.vector.scalar_tensor_tensor(out=w_rows[:], in0=probs[:], scalar=inverse[:], in1=factors[n][:],
+            nc.vector.scalar_tensor_tensor(out=w_rows[:], in0=probs, scalar=inverse[:], in1=factors[n][:],
                                            op0=ALU.mult, op1=ALU.mult)
             turn_pairs(w_rows[:], grouped)
 
@@ -123,63 +125,67 @@ def tile_attend_nsa_branches_kernel(tc, query, ckey, cval, keys_words, keys_scal
             turn_pairs(picked[:], grouped)
 
         q_mx = quantize(interleave([(on_vector, q_raw, 0, Q)], "q_grp"), "q")
-        ck_grp = interleave([(on_vector, ck_raw, 0, HALF), (on_scalar, ck_raw, HALF, N)], "ck_grp")
-        for n, (g, f) in enumerate(((gc, cf), (gs, size), (gw, mf))):
-            r0 = VEC_ROW0 + 5 * n
-            nc.scalar.dma_start(out=vec_rows[r0 : r0 + 4, :], in_=f.rearrange("o (r n) -> (o r) n", n=P))
-            nc.scalar.dma_start(out=vec_rows[r0 + 4 : r0 + 5, :], in_=g.rearrange("q o -> o q"))
-        ck_mx = quantize(ck_grp, "ck")
-        sk_scales = sbuf([P, I], U8, "sk_scales")
-        sk_codes = sbuf([P, I], U32, "sk_codes")
-        nc.vector.tensor_copy(out=sk_scales[:], in_=key_scales[:].indirect(offsets[:]))
-        nc.vector.tensor_copy(out=sk_codes[:], in_=key_words[:].indirect(offsets[:]))
-        wk_grp = interleave([(on_vector, wk_raw, 0, HALF), (on_scalar, wk_raw, HALF, N)], "wk_grp")
-        soft_c = softmax(0, ck_mx)
-        soft_s = softmax(1, (sk_codes[:], sk_scales[:]), "wk_raw")
+        gates = []
+        for n, g in enumerate((gc, gs, gw)):
+            gate = sbuf([P, 1], F32, "gate%d" % n)
+            nc.scalar.dma_start(out=gate[:], in_=g)
+            gates.append(gate)
 
         vec_turned = psum.tile([P, P], F32, name="vec_turned", tag="turn", bufs=3)
         nc.tensor.transpose(vec_turned[:], vec_rows[:], ident[:])
-        vec_cols = sbuf([P, 16], F32, "vec_cols")
-        nc.scalar.copy(out=vec_cols[:], in_=vec_turned[:, VEC_ROW0 : VEC_ROW0 + 16])
+        vec_cols = sbuf([P, 3 * PACK], F32, "vec_cols")
+        nc.vector.tensor_copy(out=vec_cols[:], in_=vec_turned[:, VEC_ROW0 : VEC_ROW0 + 3 * PACK])
+        ck_grp = interleave([(on_vector, ck_raw, 0, HALF), (on_scalar, ck_raw, HALF, N)], "ck_grp", "vec_rows")
         factors = []
         for n in range(3):
             spread = psum.tile([P, PACK, P], F32, name="spread%d" % n, tag="acc%d" % n)
             for t in range(PACK):
-                nc.tensor.transpose(spread[:, t, :], vec_cols[:, 5 * n + t : 5 * n + t + 1].to_broadcast([P, P]),
-                                    ident[:])
+                col = PACK * n + t
+                nc.tensor.transpose(spread[:, t, :], vec_cols[:, col : col + 1].to_broadcast([P, P]), ident[:])
             factor = sbuf([P, N], F32, "factor%d" % n)
             nc.scalar.activation(out=factor[:], in_=spread[:].rearrange("p t s -> p (t s)"), func=ACT.Copy,
-                                 scale=vec_cols[:, 5 * n + 4 : 5 * n + 5])
+                                 scale=gates[n][:])
             factors.append(factor)
 
+        ck_mx = quantize(ck_grp, "ck")
+        sk_scales = sbuf([P, I], U8, "sk_scales", "ck_raw")
+        sk_codes = sbuf([P, I], U32, "sk_codes", "vec_rows")
+        nc.vector.tensor_copy(out=sk_scales[:], in_=key_scales[:].indirect(offsets[:]))
+        nc.vector.tensor_copy(out=sk_codes[:], in_=key_words[:].indirect(offsets[:]))
+        wk_grp = interleave([(on_scalar, wk_raw, 0, HALF), (on_scalar, wk_raw, HALF, N)], "wk_grp")
+        probs_cs = sbuf([P, 2, N], F32, "probs_cs", "wk_raw")
+        soft_c = softmax(0, ck_mx, probs_cs[:, 0, :])
+        soft_s = softmax(1, (sk_codes[:], sk_scales[:]), probs_cs[:, 1, :])
+
         first = sbuf([P, 4 * P, PACK], BF16, "first")
-        second = sbuf([P, 2 * P, PACK], BF16, "second")
         weigh(1, *soft_s, first[:, P : 2 * P, :])
-        soft_w = softmax(2, quantize(wk_grp, "wk"))
+        soft_w = softmax(2, quantize(wk_grp, "wk", sbuf([P, N], U32, "wk_codes", "vals0")[:]),
+                         sbuf([P, N], F32, "probs_w")[:])
 
         gather_values(0, first[:, 2 * P : 3 * P, :])
         weigh(0, *soft_c, first[:, 0:P, :])
         gather_values(1, first[:, 3 * P : 4 * P, :])
+        second = sbuf([P, 2 * P, PACK], BF16, "second", "cv_raw0")
         gather_values(2, second[:, P : 2 * P, :])
-        first_mx = quantize(first, "first", sbuf([P, 4 * P], U32, "first_codes", "vals2")[:])
+        first_mx = quantize(first, "first", sbuf([P, 4 * P], U32, "first_codes", "vals3")[:])
         weigh(2, *soft_w, second[:, 0:P, :])
         cv_grp0 = interleave([(on_scalar, cv_raw[0], 0, HALF)], "cv_grp0")
-        third = sbuf([P, P, PACK], BF16, "third", "cv_raw0")
+        third = sbuf([P, P, PACK], BF16, "third", "cv_raw%d" % HALF)
         gather_values(3, third[:])
-        second_mx = quantize(second, "second", sbuf([P, 2 * P], U32, "second_codes", "vals3")[:])
+        second_mx = quantize(second, "second")
+        third_mx = quantize(third, "third")
         wc_mx, ws_mx, ww_mx = columns(first_mx, 0, P), columns(first_mx, P, 2 * P), columns(second_mx, 0, P)
-        vt_mx = [columns(first_mx, 2 * P, 4 * P), columns(second_mx, P, 2 * P), quantize(third, "third")]
 
         accs = [psum.tile([P, c1 - c0], F32, name="acc%d" % k, tag="acc%d" % k)
                 for k, (c0, c1) in enumerate(OUT_CHUNKS)]
-        for acc, v_mx in zip(accs, vt_mx):
-            multiply(acc[:], ws_mx, v_mx, True, False)
-
+        multiply(accs[0][:], ws_mx, columns(first_mx, 2 * P, 4 * P), True, False)
         multiply(accs[0][:], wc_mx, quantize(cv_grp0, "cv0"), False, False)
         multiply(accs[1][:], wc_mx, quantize(interleave([(on_vector, cv_raw[1], 0, P)], "cv_grp1"), "cv1"),
-                 False, False)
+                 True, False)
         multiply(accs[2][:], wc_mx, quantize(interleave([(on_scalar, cv_raw[1], P, HALF)], "cv_grp2"), "cv2"),
-                 False, False)
+                 True, False)
+        multiply(accs[1][:], ws_mx, columns(second_mx, P, 2 * P), False, False)
+        multiply(accs[2][:], ws_mx, third_mx, False, False)
 
         wv_grp = [interleave([(on_vector, wv_raw[0], 0, P), (on_scalar, wv_raw[0], P, HALF)], "wv_grp0"),
                   interleave([(on_scalar, wv_raw[1], 0, P)], "wv_grp1"),

@@ -3,8 +3,8 @@ from contextlib import ExitStack
 import concourse.mybir as mybir
 from concourse.masks import make_identity
 
-D, T, I, Q, E = 512, 2048, 512, 128, 512
-FLOPS = 6 * 2 * 512 * 128 * 512
+T, I, Q, E = 2048, 512, 128, 512
+FLOPS = 6 * 2 * 512 * Q * 512
 
 F32 = mybir.dt.float32
 BF16 = mybir.dt.bfloat16
@@ -20,7 +20,10 @@ AX = mybir.AxisListType
 P = 128
 PACK = 4
 N = 512
-HALF = 256
+HALF = N // 2
+RUN = 4
+COMPRESSED, SELECTED, WINDOW = 0, 1, 2
+TURN_BANKS = 3
 VEC_ROW0 = 8
 OUT_CHUNKS = ((0, 256), (256, 384), (384, 512))
 
@@ -38,25 +41,24 @@ def tile_attend_nsa_branches_kernel(tc, query, ckey, cval, keys_words, keys_scal
 
         def load_rows(src, c0, c1, name):
             raw = sbuf([P, PACK, c1 - c0], F32, name)
-            nc.sync.dma_start(out=raw[:], in_=src.rearrange("(p j) w -> p j w", j=PACK)[:, :, c0:c1])
+            nc.sync.dma_start(out=raw[:], in_=src.rearrange("(p t) w -> p t w", t=PACK)[:, :, c0:c1])
             return raw
 
         def interleave(pieces, name, reuses=None):
             grouped = sbuf([P, sum(c1 - c0 for copy, raw, c0, c1 in pieces), PACK], BF16, name, reuses)
-            a = 0
+            start = 0
             for copy, raw, c0, c1 in pieces:
-                copy(out=grouped[:, a : a + c1 - c0, :].rearrange("p (c i) t -> p c t i", i=4),
-                     in_=raw[:, :, c0:c1].rearrange("p t (c i) -> p c t i", i=4))
-                a = a + c1 - c0
+                copy(out=grouped[:, start : start + c1 - c0, :].rearrange("p (c i) t -> p c t i", i=RUN),
+                     in_=raw[:, :, c0:c1].rearrange("p t (c i) -> p c t i", i=RUN))
+                start = start + c1 - c0
             return grouped
 
-        def quantize(grouped, name, codes=None):
+        def quantize(grouped, name, reuses=None):
             width = grouped.shape[1]
-            if codes is None:
-                codes = sbuf([P, width], U32, name + "_codes")[:]
+            codes = sbuf([P, width], U32, name + "_codes", reuses)[:]
             scales = sbuf([P, width], U8, name + "_scales")[:]
             nc.vector.quantize_mx(out=codes.bitcast(FP8X4), scales=scales,
-                                  in_=grouped[:].rearrange("p w j -> p (w j)"))
+                                  in_=grouped[:].rearrange("p w t -> p (w t)"))
             return codes, scales
 
         def columns(mx, c0, c1):
@@ -68,39 +70,10 @@ def tile_attend_nsa_branches_kernel(tc, query, ckey, cval, keys_words, keys_scal
 
         def turn_pairs(rows_bf16, grouped):
             words = rows_bf16.bitcast(F32)
-            turned = psum.tile([P, 2, P], F32, name="turned", tag="turn", bufs=3)
+            turned = psum.tile([P, 2, P], F32, name="turned", tag="turn", bufs=TURN_BANKS)
             for u in range(2):
                 nc.tensor.transpose(turned[:, u, :], words[:, u : 2 * P : 2], ident[:])
             nc.scalar.copy(out=grouped.bitcast(F32), in_=turned[:].rearrange("p u r -> p r u"))
-
-        vec_rows = sbuf([P, P], F32, "vec_rows")
-        nc.gpsimd.memset(vec_rows[:], 0.0)
-        key_scales = sbuf([P, T], U8, "key_scales")
-        nc.gpsimd.memset(key_scales[:].bitcast(I32), 0)
-        ident = sbuf([P, P], F32, "ident")
-        make_identity(nc, ident[:])
-        for n, f in enumerate((cf, size, mf)):
-            r0 = VEC_ROW0 + PACK * n
-            nc.scalar.dma_start(out=vec_rows[r0 : r0 + PACK, :], in_=f.rearrange("o (r n) -> (o r) n", n=P))
-        for quad in range(4):
-            nc.scalar.dma_start(out=key_scales[32 * quad : 32 * quad + 4, :].bitcast(I32),
-                                in_=keys_scales[0, 4 * quad : 4 * quad + 4, :].bitcast(I32))
-
-        q_raw = load_rows(query, 0, Q, "q_raw")
-        offsets = keep.tile([P, I // 16], U16, name="offsets")
-        nc.sync.dma_start(offsets[:], offs)
-        ck_raw = load_rows(ckey, 0, N, "ck_raw")
-        key_words = sbuf([P, T], U32, "key_words")
-        nc.sync.dma_start(out=key_words[:].bitcast(I32),
-                          in_=keys_words[0].rearrange("p n t -> p (n t)").bitcast(I32))
-        wk_raw = load_rows(wkey, 0, N, "wk_raw")
-        pools = []
-        for b in range(E // P):
-            pool_b = sbuf([P, T], F32, "vals%d" % b)
-            nc.sync.dma_start(out=pool_b[:], in_=vals[b * P : (b + 1) * P, :])
-            pools.append(pool_b)
-        cv_raw = [load_rows(cval, c0, c0 + HALF, "cv_raw%d" % c0) for c0 in (0, HALF)]
-        wv_raw = [load_rows(wval, c0, c1, "wv_raw%d" % c0) for c0, c1 in OUT_CHUNKS]
 
         def softmax(n, keys_mx, probs):
             scores = psum.tile([P, N], F32, name="scores%d" % n, tag="scores", bufs=2)
@@ -121,17 +94,46 @@ def tile_attend_nsa_branches_kernel(tc, query, ckey, cval, keys_words, keys_scal
 
         def gather_values(b, grouped):
             picked = sbuf([P, I], BF16, "picked%d" % b)
-            nc.vector.tensor_copy(out=picked[:], in_=pools[b][:].indirect(offsets[:]))
+            nc.vector.tensor_copy(out=picked[:], in_=value_pools[b][:].indirect(offsets[:]))
             turn_pairs(picked[:], grouped)
+
+        vec_rows = sbuf([P, P], F32, "vec_rows")
+        nc.gpsimd.memset(vec_rows[:], 0.0)
+        key_scales = sbuf([P, T], U8, "key_scales")
+        nc.gpsimd.memset(key_scales[:].bitcast(I32), 0)
+        ident = sbuf([P, P], F32, "ident")
+        make_identity(nc, ident[:])
+        for n, factor_row in enumerate((cf, size, mf)):
+            r0 = VEC_ROW0 + PACK * n
+            nc.scalar.dma_start(out=vec_rows[r0 : r0 + PACK, :],
+                                in_=factor_row.rearrange("o (r c) -> (o r) c", c=P))
+        for quad in range(4):
+            nc.scalar.dma_start(out=key_scales[32 * quad : 32 * quad + 4, :].bitcast(I32),
+                                in_=keys_scales[0, 4 * quad : 4 * quad + 4, :].bitcast(I32))
+
+        q_raw = load_rows(query, 0, Q, "q_raw")
+        offsets = keep.tile([P, I // 16], U16, name="offsets")
+        nc.sync.dma_start(offsets[:], offs)
+        ck_raw = load_rows(ckey, 0, N, "ck_raw")
+        key_words = sbuf([P, T], U32, "key_words")
+        nc.sync.dma_start(out=key_words[:].bitcast(I32),
+                          in_=keys_words[0].rearrange("p n t -> p (n t)").bitcast(I32))
+        wk_raw = load_rows(wkey, 0, N, "wk_raw")
+        value_pools = []
+        for b in range(E // P):
+            value_pool = sbuf([P, T], F32, "vals%d" % b)
+            nc.sync.dma_start(out=value_pool[:], in_=vals[b * P : (b + 1) * P, :])
+            value_pools.append(value_pool)
+        cv_raw = load_rows(cval, 0, E, "cv_raw")
+        wv_raw = [load_rows(wval, c0, c1, "wv_raw%d" % c0) for c0, c1 in OUT_CHUNKS]
 
         q_mx = quantize(interleave([(on_vector, q_raw, 0, Q)], "q_grp"), "q")
         gates = []
-        for n, g in enumerate((gc, gs, gw)):
+        for n, gate_col in enumerate((gc, gs, gw)):
             gate = sbuf([P, 1], F32, "gate%d" % n)
-            nc.scalar.dma_start(out=gate[:], in_=g)
+            nc.scalar.dma_start(out=gate[:], in_=gate_col)
             gates.append(gate)
-
-        vec_turned = psum.tile([P, P], F32, name="vec_turned", tag="turn", bufs=3)
+        vec_turned = psum.tile([P, P], F32, name="vec_turned", tag="turn", bufs=TURN_BANKS)
         nc.tensor.transpose(vec_turned[:], vec_rows[:], ident[:])
         vec_cols = sbuf([P, 3 * PACK], F32, "vec_cols")
         nc.vector.tensor_copy(out=vec_cols[:], in_=vec_turned[:, VEC_ROW0 : VEC_ROW0 + 3 * PACK])
@@ -139,11 +141,11 @@ def tile_attend_nsa_branches_kernel(tc, query, ckey, cval, keys_words, keys_scal
         factors = []
         for n in range(3):
             spread = psum.tile([P, PACK, P], F32, name="spread%d" % n, tag="acc%d" % n)
-            for t in range(PACK):
-                col = PACK * n + t
-                nc.tensor.transpose(spread[:, t, :], vec_cols[:, col : col + 1].to_broadcast([P, P]), ident[:])
+            for r in range(PACK):
+                col = PACK * n + r
+                nc.tensor.transpose(spread[:, r, :], vec_cols[:, col : col + 1].to_broadcast([P, P]), ident[:])
             factor = sbuf([P, N], F32, "factor%d" % n)
-            nc.scalar.activation(out=factor[:], in_=spread[:].rearrange("p t s -> p (t s)"), func=ACT.Copy,
+            nc.scalar.activation(out=factor[:], in_=spread[:].rearrange("p r c -> p (r c)"), func=ACT.Copy,
                                  scale=gates[n][:])
             factors.append(factor)
 
@@ -154,37 +156,36 @@ def tile_attend_nsa_branches_kernel(tc, query, ckey, cval, keys_words, keys_scal
         nc.vector.tensor_copy(out=sk_codes[:], in_=key_words[:].indirect(offsets[:]))
         wk_grp = interleave([(on_scalar, wk_raw, 0, HALF), (on_scalar, wk_raw, HALF, N)], "wk_grp")
         probs_cs = sbuf([P, 2, N], F32, "probs_cs", "wk_raw")
-        soft_c = softmax(0, ck_mx, probs_cs[:, 0, :])
-        soft_s = softmax(1, (sk_codes[:], sk_scales[:]), probs_cs[:, 1, :])
+        soft_c = softmax(COMPRESSED, ck_mx, probs_cs[:, 0, :])
+        soft_s = softmax(SELECTED, (sk_codes[:], sk_scales[:]), probs_cs[:, 1, :])
 
         first = sbuf([P, 4 * P, PACK], BF16, "first")
-        weigh(1, *soft_s, first[:, P : 2 * P, :])
-        soft_w = softmax(2, quantize(wk_grp, "wk", sbuf([P, N], U32, "wk_codes", "vals0")[:]),
-                         sbuf([P, N], F32, "probs_w")[:])
+        weigh(SELECTED, *soft_s, first[:, P : 2 * P, :])
+        wk_mx = quantize(wk_grp, "wk", "vals0")
+        soft_w = softmax(WINDOW, wk_mx, sbuf([P, N], F32, "probs_w")[:])
 
         gather_values(0, first[:, 2 * P : 3 * P, :])
-        weigh(0, *soft_c, first[:, 0:P, :])
+        weigh(COMPRESSED, *soft_c, first[:, 0:P, :])
         gather_values(1, first[:, 3 * P : 4 * P, :])
-        second = sbuf([P, 2 * P, PACK], BF16, "second", "cv_raw0")
+        second = sbuf([P, 2 * P, PACK], BF16, "second")
         gather_values(2, second[:, P : 2 * P, :])
-        first_mx = quantize(first, "first", sbuf([P, 4 * P], U32, "first_codes", "vals3")[:])
-        weigh(2, *soft_w, second[:, 0:P, :])
-        cv_grp0 = interleave([(on_scalar, cv_raw[0], 0, HALF)], "cv_grp0")
-        third = sbuf([P, P, PACK], BF16, "third", "cv_raw%d" % HALF)
+        first_mx = quantize(first, "first", "vals2")
+        weigh(WINDOW, *soft_w, second[:, 0:P, :])
+        cv_low = interleave([(on_scalar, cv_raw, 0, HALF)], "cv_low")
+        third = sbuf([P, P, PACK], BF16, "third", "cv_raw")
         gather_values(3, third[:])
-        second_mx = quantize(second, "second")
+        second_mx = quantize(second, "second", "vals3")
         third_mx = quantize(third, "third")
         wc_mx, ws_mx, ww_mx = columns(first_mx, 0, P), columns(first_mx, P, 2 * P), columns(second_mx, 0, P)
 
         accs = [psum.tile([P, c1 - c0], F32, name="acc%d" % k, tag="acc%d" % k)
                 for k, (c0, c1) in enumerate(OUT_CHUNKS)]
         multiply(accs[0][:], ws_mx, columns(first_mx, 2 * P, 4 * P), True, False)
-        multiply(accs[0][:], wc_mx, quantize(cv_grp0, "cv0"), False, False)
-        multiply(accs[1][:], wc_mx, quantize(interleave([(on_vector, cv_raw[1], 0, P)], "cv_grp1"), "cv1"),
-                 True, False)
-        multiply(accs[2][:], wc_mx, quantize(interleave([(on_scalar, cv_raw[1], P, HALF)], "cv_grp2"), "cv2"),
-                 True, False)
-        multiply(accs[1][:], ws_mx, columns(second_mx, P, 2 * P), False, False)
+        multiply(accs[1][:], ws_mx, columns(second_mx, P, 2 * P), True, False)
+        cv_high_mx = quantize(interleave([(on_vector, cv_raw, HALF, E)], "cv_high"), "cv_high")
+        multiply(accs[1][:], wc_mx, columns(cv_high_mx, 0, P), False, False)
+        multiply(accs[2][:], wc_mx, columns(cv_high_mx, P, 2 * P), True, False)
+        multiply(accs[0][:], wc_mx, quantize(cv_low, "cv_low"), False, False)
         multiply(accs[2][:], ws_mx, third_mx, False, False)
 
         wv_grp = [interleave([(on_vector, wv_raw[0], 0, P), (on_scalar, wv_raw[0], P, HALF)], "wv_grp0"),

from contextlib import ExitStack

import concourse.mybir as mybir
from concourse.masks import make_identity

T, I, Q, E = 2048, 512, 128, 512
FLOPS = 6 * 2 * 512 * Q * 512

F32 = mybir.dt.float32
BF16 = mybir.dt.bfloat16
I32 = mybir.dt.int32
U32 = mybir.dt.uint32
U16 = mybir.dt.uint16
U8 = mybir.dt.uint8
FP8X4 = mybir.dt.float8_e4m3fn_x4
ALU = mybir.AluOpType
ACT = mybir.ActivationFunctionType
AX = mybir.AxisListType

P = 128
PACK = 4
N = 512
HALF = N // 2
RUN = 4
COMPRESSED, SELECTED, WINDOW = 0, 1, 2
TURN_BANKS = 3
VEC_ROW0 = 8
OUT_CHUNKS = ((0, 256), (256, 384), (384, 512))


def tile_attend_nsa_branches_kernel(tc, query, ckey, cval, keys_words, keys_scales, vals, wkey, wval,
                                     gc, gs, gw, cf, size, mf, offs, out):
    nc = tc.nc
    with ExitStack() as ctx:
        keep = ctx.enter_context(tc.tile_pool(name="keep", bufs=1))
        psum = ctx.enter_context(tc.psum_pool(name="psum", bufs=1))
        on_vector, on_scalar = nc.vector.tensor_copy, nc.scalar.copy

        def sbuf(shape, dtype, name, reuses=None):
            return keep.tile(shape, dtype, name=name, tag=reuses or name, align_bytes=64)

        def load_rows(src, c0, c1, name):
            raw = sbuf([P, PACK, c1 - c0], F32, name)
            nc.sync.dma_start(out=raw[:], in_=src.rearrange("(p t) w -> p t w", t=PACK)[:, :, c0:c1])
            return raw

        def interleave(pieces, name, reuses=None):
            grouped = sbuf([P, sum(c1 - c0 for copy, raw, c0, c1 in pieces), PACK], BF16, name, reuses)
            start = 0
            for copy, raw, c0, c1 in pieces:
                copy(out=grouped[:, start : start + c1 - c0, :].rearrange("p (c i) t -> p c t i", i=RUN),
                     in_=raw[:, :, c0:c1].rearrange("p t (c i) -> p c t i", i=RUN))
                start = start + c1 - c0
            return grouped

        def quantize(grouped, name, reuses=None):
            width = grouped.shape[1]
            codes = sbuf([P, width], U32, name + "_codes", reuses)[:]
            scales = sbuf([P, width], U8, name + "_scales")[:]
            nc.vector.quantize_mx(out=codes.bitcast(FP8X4), scales=scales,
                                  in_=grouped[:].rearrange("p w t -> p (w t)"))
            return codes, scales

        def columns(mx, c0, c1):
            return mx[0][:, c0:c1], mx[1][:, c0:c1]

        def multiply(acc, lhs, rhs, start, stop):
            nc.tensor.matmul_mx(out=acc, lhsT=lhs[0].bitcast(FP8X4), lhsT_scale=lhs[1],
                                rhs=rhs[0].bitcast(FP8X4), rhs_scale=rhs[1], start=start, stop=stop)

        def turn_pairs(rows_bf16, grouped):
            words = rows_bf16.bitcast(F32)
            turned = psum.tile([P, 2, P], F32, name="turned", tag="turn", bufs=TURN_BANKS)
            for u in range(2):
                nc.tensor.transpose(turned[:, u, :], words[:, u : 2 * P : 2], ident[:])
            nc.scalar.copy(out=grouped.bitcast(F32), in_=turned[:].rearrange("p u r -> p r u"))

        def softmax(n, keys_mx, probs):
            scores = psum.tile([P, N], F32, name="scores%d" % n, tag="scores", bufs=2)
            multiply(scores[:], q_mx, keys_mx, True, True)
            neg_max = sbuf([P, 1], F32, "neg_max%d" % n)
            nc.vector.tensor_reduce(out=neg_max[:], in_=scores[:], axis=AX.X, op=ALU.max, negate=True)
            total = sbuf([P, 1], F32, "total%d" % n)
            nc.scalar.activation(out=probs, in_=scores[:], func=ACT.Exp, bias=neg_max[:], accum_out=total[:])
            inverse = sbuf([P, 1], F32, "inverse%d" % n)
            nc.vector.reciprocal(out=inverse[:], in_=total[:])
            return probs, inverse

        def weigh(n, probs, inverse, grouped):
            w_rows = sbuf([P, N], BF16, "w_rows%d" % n)
            nc.vector.scalar_tensor_tensor(out=w_rows[:], in0=probs, scalar=inverse[:], in1=factors[n][:],
                                           op0=ALU.mult, op1=ALU.mult)
            turn_pairs(w_rows[:], grouped)

        def gather_values(b, grouped):
            picked = sbuf([P, I], BF16, "picked%d" % b)
            nc.vector.tensor_copy(out=picked[:], in_=value_pools[b][:].indirect(offsets[:]))
            turn_pairs(picked[:], grouped)

        vec_rows = sbuf([P, P], F32, "vec_rows")
        nc.gpsimd.memset(vec_rows[:], 0.0)
        key_scales = sbuf([P, T], U8, "key_scales")
        nc.gpsimd.memset(key_scales[:].bitcast(I32), 0)
        ident = sbuf([P, P], F32, "ident")
        make_identity(nc, ident[:])
        for n, factor_row in enumerate((cf, size, mf)):
            r0 = VEC_ROW0 + PACK * n
            nc.scalar.dma_start(out=vec_rows[r0 : r0 + PACK, :],
                                in_=factor_row.rearrange("o (r c) -> (o r) c", c=P))
        for quad in range(4):
            nc.scalar.dma_start(out=key_scales[32 * quad : 32 * quad + 4, :].bitcast(I32),
                                in_=keys_scales[0, 4 * quad : 4 * quad + 4, :].bitcast(I32))

        q_raw = load_rows(query, 0, Q, "q_raw")
        offsets = keep.tile([P, I // 16], U16, name="offsets")
        nc.sync.dma_start(offsets[:], offs)
        ck_raw = load_rows(ckey, 0, N, "ck_raw")
        key_words = sbuf([P, T], U32, "key_words")
        nc.sync.dma_start(out=key_words[:].bitcast(I32),
                          in_=keys_words[0].rearrange("p n t -> p (n t)").bitcast(I32))
        wk_raw = load_rows(wkey, 0, N, "wk_raw")
        value_pools = []
        for b in range(E // P):
            value_pool = sbuf([P, T], F32, "vals%d" % b)
            nc.sync.dma_start(out=value_pool[:], in_=vals[b * P : (b + 1) * P, :])
            value_pools.append(value_pool)
        cv_raw = load_rows(cval, 0, E, "cv_raw")
        wv_raw = [load_rows(wval, c0, c1, "wv_raw%d" % c0) for c0, c1 in OUT_CHUNKS]

        q_mx = quantize(interleave([(on_vector, q_raw, 0, Q)], "q_grp"), "q")
        gates = []
        for n, gate_col in enumerate((gc, gs, gw)):
            gate = sbuf([P, 1], F32, "gate%d" % n)
            nc.scalar.dma_start(out=gate[:], in_=gate_col)
            gates.append(gate)
        vec_turned = psum.tile([P, P], F32, name="vec_turned", tag="turn", bufs=TURN_BANKS)
        nc.tensor.transpose(vec_turned[:], vec_rows[:], ident[:])
        vec_cols = sbuf([P, 3 * PACK], F32, "vec_cols")
        nc.vector.tensor_copy(out=vec_cols[:], in_=vec_turned[:, VEC_ROW0 : VEC_ROW0 + 3 * PACK])
        ck_grp = interleave([(on_vector, ck_raw, 0, HALF), (on_scalar, ck_raw, HALF, N)], "ck_grp", "vec_rows")
        factors = []
        for n in range(3):
            spread = psum.tile([P, PACK, P], F32, name="spread%d" % n, tag="acc%d" % n)
            for r in range(PACK):
                col = PACK * n + r
                nc.tensor.transpose(spread[:, r, :], vec_cols[:, col : col + 1].to_broadcast([P, P]), ident[:])
            factor = sbuf([P, N], F32, "factor%d" % n)
            nc.scalar.activation(out=factor[:], in_=spread[:].rearrange("p r c -> p (r c)"), func=ACT.Copy,
                                 scale=gates[n][:])
            factors.append(factor)

        ck_mx = quantize(ck_grp, "ck")
        sk_scales = sbuf([P, I], U8, "sk_scales", "ck_raw")
        sk_codes = sbuf([P, I], U32, "sk_codes", "vec_rows")
        nc.vector.tensor_copy(out=sk_scales[:], in_=key_scales[:].indirect(offsets[:]))
        nc.vector.tensor_copy(out=sk_codes[:], in_=key_words[:].indirect(offsets[:]))
        wk_grp = interleave([(on_scalar, wk_raw, 0, HALF), (on_scalar, wk_raw, HALF, N)], "wk_grp")
        probs_cs = sbuf([P, 2, N], F32, "probs_cs", "wk_raw")
        soft_c = softmax(COMPRESSED, ck_mx, probs_cs[:, 0, :])
        soft_s = softmax(SELECTED, (sk_codes[:], sk_scales[:]), probs_cs[:, 1, :])

        first = sbuf([P, 4 * P, PACK], BF16, "first")
        weigh(SELECTED, *soft_s, first[:, P : 2 * P, :])
        wk_mx = quantize(wk_grp, "wk", "vals0")
        soft_w = softmax(WINDOW, wk_mx, sbuf([P, N], F32, "probs_w")[:])

        gather_values(0, first[:, 2 * P : 3 * P, :])
        weigh(COMPRESSED, *soft_c, first[:, 0:P, :])
        gather_values(1, first[:, 3 * P : 4 * P, :])
        second = sbuf([P, 2 * P, PACK], BF16, "second")
        gather_values(2, second[:, P : 2 * P, :])
        first_mx = quantize(first, "first", "vals2")
        weigh(WINDOW, *soft_w, second[:, 0:P, :])
        cv_low = interleave([(on_scalar, cv_raw, 0, HALF)], "cv_low")
        third = sbuf([P, P, PACK], BF16, "third", "cv_raw")
        gather_values(3, third[:])
        second_mx = quantize(second, "second", "vals3")
        third_mx = quantize(third, "third")
        wc_mx, ws_mx, ww_mx = columns(first_mx, 0, P), columns(first_mx, P, 2 * P), columns(second_mx, 0, P)

        accs = [psum.tile([P, c1 - c0], F32, name="acc%d" % k, tag="acc%d" % k)
                for k, (c0, c1) in enumerate(OUT_CHUNKS)]
        multiply(accs[0][:], ws_mx, columns(first_mx, 2 * P, 4 * P), True, False)
        multiply(accs[1][:], ws_mx, columns(second_mx, P, 2 * P), True, False)
        cv_high_mx = quantize(interleave([(on_vector, cv_raw, HALF, E)], "cv_high"), "cv_high")
        multiply(accs[1][:], wc_mx, columns(cv_high_mx, 0, P), False, False)
        multiply(accs[2][:], wc_mx, columns(cv_high_mx, P, 2 * P), True, False)
        multiply(accs[0][:], wc_mx, quantize(cv_low, "cv_low"), False, False)
        multiply(accs[2][:], ws_mx, third_mx, False, False)

        wv_grp = [interleave([(on_vector, wv_raw[0], 0, P), (on_scalar, wv_raw[0], P, HALF)], "wv_grp0"),
                  interleave([(on_scalar, wv_raw[1], 0, P)], "wv_grp1"),
                  interleave([(on_vector, wv_raw[2], 0, P)], "wv_grp2")]
        wv_mx = [quantize(grouped, "wv%d" % k) for k, grouped in enumerate(wv_grp)]
        for acc, v_mx, (c0, c1) in zip(accs, wv_mx, OUT_CHUNKS):
            multiply(acc[:], ww_mx, v_mx, False, True)
            result = sbuf([P, c1 - c0], F32, "result%d" % c0)
            nc.scalar.copy(out=result[:], in_=acc[:])
            nc.sync.dma_start(out=out[:, c0:c1], in_=result[:])
